import numpy as np
import ml_dtypes


def mxq(x, axis, fmt="e4m3"):
    dtype, down = {"e4m3": (ml_dtypes.float8_e4m3fn, 7), "e5m2": (ml_dtypes.float8_e5m2, 14)}[fmt]
    v = np.moveaxis(np.asarray(x, np.float32).astype(ml_dtypes.bfloat16).astype(np.float64), axis, -1)
    blocks = v.reshape(v.shape[:-1] + (-1, 32))
    amax = np.abs(blocks).max(-1, keepdims=True)
    byte = np.maximum(np.where(amax > 0, np.frexp(amax)[1] - 1 + 127, 0) - down, 1)
    scale = np.exp2(byte - 127.0)
    codes = (blocks / scale).astype(np.float32).astype(dtype).astype(np.float64)
    return np.moveaxis((codes * scale).reshape(v.shape), -1, axis)


WIDE = False


def mx_kscale(k):
    if not WIDE:
        return np.ones(k)
    levels = np.array([10, -10, 5, -5, 0])
    if k % 512:
        return np.exp2(np.random.permutation(np.resize(levels, k // 32))).repeat(32)
    a = np.empty((k // 512, 16))
    for p in range(k // 512):
        a[p, :8] = np.random.permutation(np.resize(levels, 8))
        for g in range(8):
            far = levels[np.abs(levels - a[p, g]) >= 10]
            a[p, g + 8] = far[np.random.randint(len(far))]
    return np.exp2(a.ravel()).repeat(32)


def f64(x):
    return np.asarray(x).astype(np.float64)


def striped(idx):
    return np.tile(idx.reshape(-1, 16).T, (8, 1)).astype(np.uint16)


def unstriped(offs):
    return offs[:16].T.reshape(-1).astype(np.int64)


def pack_weight(w):
    k, n = w.shape
    w = f64(np.asarray(w, np.float32).astype(ml_dtypes.bfloat16)).reshape(k // 32, 32, n)
    amax = np.abs(w).max(1)
    byte = np.clip(np.where(amax > 0, np.frexp(amax)[1] - 1 + 127 - 7, 1), 1, 254)
    scaled = (w * np.exp2(127.0 - byte)[:, None, :]).reshape(k, n).astype(np.float32)
    words = np.ascontiguousarray(scaled.reshape(k // 512, 128, 4, n).transpose(0, 1, 3, 2)).astype(ml_dtypes.float8_e4m3fn).view(np.uint8)
    return words, np.ascontiguousarray(byte.astype(np.uint8).reshape(k // 512, 16, n))


def unpack_weight(words, scales):
    g, p, n, _ = words.shape
    vals = np.ascontiguousarray(words).view(ml_dtypes.float8_e4m3fn).astype(np.float64) * np.repeat(np.exp2(scales.astype(np.float64) - 127.0), 8, axis=1)[..., None]
    return vals.transpose(0, 1, 3, 2).reshape(g * 512, n)


def sigmoid(v):
    return 1.0 / (1.0 + np.exp(-np.maximum(v, -700.0)))


K, T, S, D, H, Z, W = 512, 2048, 512, 2, 512, 512, 2048
P = 2 ** 7


def setup_inputs():
    n = np.random.standard_normal
    s = mx_kscale(K)[:, None]
    packed_xT = pack_weight(n((K, T)) * s)
    packed_eT = pack_weight(n((K, W)) * s)
    return {
        "x_words": packed_xT[0],
        "x_scales": packed_xT[1],
        "w1": (n((K, H)) / np.sqrt(K) / s).astype(np.float32),
        "w2": (n((K, H)) / np.sqrt(K) / s).astype(np.float32),
        "e_words": packed_eT[0],
        "e_scales": packed_eT[1],
        "unit": (np.random.uniform(0.6, 1.4, (K, 1)) / np.sqrt(K) / s).astype(np.float32),
        "mth": (np.tile(np.random.uniform(0.3, 1.3, W), (P, 1))).astype(np.float32),
        "offs": striped(np.random.permutation(T)[:S]),
        "syn": striped(np.random.permutation(S)),
        "adk": striped(np.random.permutation(W)[:Z]),
        "brd": striped(np.random.permutation(Z)),
    }


def reference(x_words, x_scales, w1, w2, e_words, e_scales, unit, mth, offs, syn, adk, brd):
    xq = unpack_weight(x_words, x_scales)[:, unstriped(offs)]
    y = mxq(f64(w1), 0, "e4m3").T @ xq
    yg = mxq(f64(w2), 0, "e4m3").T @ xq
    gs = yg[:, unstriped(syn)]
    bst = np.maximum(y, gs)
    aw = bst * np.abs(y)
    qv = aw.reshape(len(aw), -1, D).sum(axis=2)
    sat = qv / (np.sqrt((qv) ** 2 + 0.5))
    hid = f64(unit) * sat
    e_adk = unpack_weight(e_words, e_scales)[:, unstriped(adk)]
    sc = mxq(hid, 0, "e4m3").T @ e_adk
    grp4 = sc.reshape(len(sc), -1, 4).mean(axis=2)
    excl = sc - (0.8 * np.repeat(grp4, 4, axis=1))
    xm = excl * (f64(mth)[:1][:, unstriped(adk)])
    sb_ = sc[:, unstriped(brd)]
    return sigmoid(xm) * sb_

@@ -1,0 +1,260 @@
+from contextlib import ExitStack
+
+import concourse.mybir as mybir
+
+F32 = mybir.dt.float32
+BF16 = mybir.dt.bfloat16
+I32 = mybir.dt.int32
+U32 = mybir.dt.uint32
+U16 = mybir.dt.uint16
+U8 = mybir.dt.uint8
+FP8X4 = mybir.dt.float8_e4m3fn_x4
+ALU = mybir.AluOpType
+ACT = mybir.ActivationFunctionType
+AX = mybir.AxisListType
+
+P = 128
+PACK = 4
+K = 512
+TABLE = 2048
+S = 512
+H = 512
+Z = 512
+V = 256
+HALF = S // 2
+FLOPS = 2 * K * H * S * 2 + 2 * H * V * Z
+
+
+def tile_picked_ysponsq_brd_p_kernel(
+    tc, x_words, x_scales, w1, w2, e_words, e_scales, unit, mth, offs, syn, adk, brd, out
+):
+    nc = tc.nc
+    with ExitStack() as ctx:
+        keep = ctx.enter_context(tc.tile_pool(name="keep", bufs=1))
+        psum = ctx.enter_context(tc.psum_pool(name="psum", bufs=1))
+
+        def load_list(name, src):
+            t = keep.tile([P, S // 16], U16, name=name)
+            nc.sync.dma_start(t[:], src)
+            return t
+
+        def load_words(name, src):
+            t = keep.tile([P, TABLE], U32, name=name)
+            nc.sync.dma_start(t[:].bitcast(I32), src[0].rearrange("p n t -> p (n t)").bitcast(I32))
+            return t
+
+        def load_weight(name, src):
+            parts = []
+            rows = src.rearrange("(p j) c -> p j c", j=PACK)
+            for c in range(2):
+                t = keep.tile([P, PACK, H // 2], F32, name=name + str(c))
+                nc.sync.dma_start(t[:], rows[:, :, c * (H // 2) : (c + 1) * (H // 2)])
+                parts.append(t)
+            return parts
+
+        def cast_weight(dealt, part, c, copy):
+            src = part[:].rearrange("p j (m t) -> p m j t", t=PACK)
+            dst = dealt[:, :, c * 64 : (c + 1) * 64, :].rearrange("p t m j -> p m j t")
+            copy(dst, src)
+
+        def quantise(name, src, width, pieces):
+            codes = keep.tile([P, width], U32, name=name + "_c", align_bytes=64)
+            scales = keep.tile([P, width], U8, name=name + "_s", align_bytes=64)
+            n = width // pieces
+            for i in range(pieces):
+                nc.vector.quantize_mx(
+                    out=codes[:, i * n : (i + 1) * n].bitcast(FP8X4),
+                    scales=scales[:, i * n : (i + 1) * n],
+                    in_=src[:, PACK * i * n : PACK * (i + 1) * n],
+                )
+            return codes, scales
+
+        def gather(name, table, offsets, dtype):
+            t = keep.tile([P, S], dtype, name=name, align_bytes=64)
+            nc.vector.tensor_copy(t[:], table[:].indirect(offsets[:]))
+            return t
+
+        def product(dst, lhs, lhs_cols, rhs, rhs_cols):
+            nc.tensor.matmul_mx(
+                out=dst,
+                lhsT=lhs[0][:, lhs_cols].bitcast(FP8X4),
+                lhsT_scale=lhs[1][:, lhs_cols],
+                rhs=rhs[0][:, rhs_cols].bitcast(FP8X4),
+                rhs_scale=rhs[1][:, rhs_cols],
+                start=True,
+                stop=True,
+            )
+
+        def block(i, n):
+            return slice(i * n, (i + 1) * n)
+
+        def load_scales(name, src):
+            t = keep.tile([P, TABLE], U8, name=name)
+            for q in range(4):
+                rows = src[0, block(q, 4), :].bitcast(I32).partition_broadcast(8)
+                nc.sync.dma_start(t[block(q, 32), :].bitcast(I32), rows)
+            return t
+
+        xs_tab = load_scales("xs_tab", x_scales)
+        offs_t = load_list("offs_t", offs)
+        x_tab = load_words("x_tab", x_words)
+        w2_raw = load_weight("w2_raw", w2)
+        w1_raw = load_weight("w1_raw", w1)
+        syn_t = load_list("syn_t", syn)
+        unit_t = keep.tile([P, PACK], F32, name="unit_t")
+        nc.sync.dma_start(unit_t[:], unit.rearrange("(p t) o -> p (t o)", t=PACK))
+        adk_t = load_list("adk_t", adk)
+        es_tab = load_scales("es_tab", e_scales)
+        e_tab = load_words("e_tab", e_words)
+        mth_tab = keep.tile([P, TABLE], F32, name="mth_tab")
+        nc.sync.dma_start(mth_tab[:], mth)
+        brd_t = load_list("brd_t", brd)
+
+        half_c = keep.tile([P, 1], F32, name="half_c")
+        nc.vector.memset(half_c[:], 0.5)
+
+        xq_s = gather("xq_s", xs_tab, offs_t, U8)
+        xq = (gather("xq", x_tab, offs_t, U32), xq_s)
+
+        w2_b = keep.tile([P, PACK, P, PACK], BF16, name="w2_b", align_bytes=64)
+        cast_weight(w2_b, w2_raw[0], 0, nc.scalar.copy)
+        cast_weight(w2_b, w2_raw[1], 1, nc.vector.tensor_copy)
+        w2_q = quantise("w2", w2_b[:].rearrange("p t m j -> p (t m j)"), H, 2)
+
+        yg_ps = [psum.tile([P, S], F32, name="yg_ps", tag="a" + str(t)) for t in range(PACK)]
+        yg_sb = [keep.tile([P, S], F32, name="yg_sb" + str(t)) for t in range(PACK)]
+        gs = [keep.tile([P, PACK, HALF], F32, name="gs" + str(h)) for h in range(2)]
+        for t in range(PACK):
+            product(yg_ps[t][:], w2_q, block(t, P), xq, block(0, S))
+
+        def fetch_syn(h, t, on_vector):
+            window = yg_sb[t][:].indirect(syn_t[:, block(h, 16)])
+            if on_vector:
+                nc.vector.tensor_copy(gs[h][:, t, :], window)
+            else:
+                nc.scalar.activation(gs[h][:, t, :], window, ACT.Copy)
+
+        w1_b = keep.tile([P, PACK, P, PACK], BF16, name="w1_b", align_bytes=64)
+        cast_weight(w1_b, w1_raw[0], 0, nc.vector.tensor_copy)
+        for t in range(PACK):
+            nc.scalar.copy(yg_sb[t][:], yg_ps[t][:])
+        fetch_syn(0, 0, True)
+        cast_weight(w1_b, w1_raw[1], 1, nc.vector.tensor_copy)
+
+        u_zero = keep.tile([P, PACK], F32, name="u_zero")
+        nc.vector.tensor_scalar(u_zero[:], unit_t[:], 0.0, None, ALU.is_equal)
+        w1_q = quantise("w1", w1_b[:].rearrange("p t m j -> p (t m j)"), H, 2)
+        u_safe = keep.tile([P, PACK], F32, name="u_safe")
+        nc.vector.tensor_tensor(u_safe[:], u_zero[:], unit_t[:], ALU.add)
+        fetch_syn(0, 1, True)
+        u_inv = keep.tile([P, PACK], F32, name="u_inv")
+        nc.vector.reciprocal(u_inv[:], u_safe[:])
+        eq_s = gather("eq_s", es_tab, adk_t, U8)
+        fetch_syn(0, 2, False)
+        fetch_syn(0, 3, False)
+
+        best = [keep.tile([P, PACK, HALF], F32, name="best" + str(h)) for h in range(2)]
+        mag = [keep.tile([P, PACK, HALF], F32, name="mag" + str(h)) for h in range(2)]
+        y_ps = [psum.tile([P, 2, HALF], F32, name="y_ps", tag="b" + str(b)) for b in range(4)]
+        for h in range(2):
+            for t in range(PACK):
+                product(y_ps[2 * h + t // 2][:, t % 2, :], w1_q, block(t, P), xq, block(h, HALF))
+
+        def magnitude(h, tt):
+            nc.scalar.activation(mag[h][:, block(tt, 2), :], y_ps[2 * h + tt][:], ACT.Abs)
+
+        def larger(h, tt):
+            nc.vector.tensor_tensor(best[h][:, block(tt, 2), :], y_ps[2 * h + tt][:], gs[h][:, block(tt, 2), :], ALU.max)
+
+        def weigh(h):
+            aw = keep.tile([P, PACK, HALF], F32, name="aw" + str(h))
+            qu = keep.tile([P, PACK, P], F32, name="qu" + str(h))
+            for t in range(PACK):
+                nc.vector.scalar_tensor_tensor(
+                    aw[:, t, :], best[h][:, t, :], unit_t[:, t : t + 1], mag[h][:, t, :], ALU.mult, ALU.mult
+                )
+            pairs = aw[:].rearrange("p t (v d) -> p t v d", d=2)
+            nc.vector.tensor_tensor(qu[:], pairs[:, :, :, 0], pairs[:, :, :, 1], ALU.add)
+            return qu
+
+        def inverse_root(h, qu):
+            sq = keep.tile([P, PACK, P], F32, name="sq" + str(h))
+            for t in range(PACK):
+                nc.scalar.activation(sq[:, t, :], qu[:, t, :], ACT.Square, scale=u_inv[:, t : t + 1])
+            root = keep.tile([P, PACK, P], F32, name="root" + str(h))
+            nc.scalar.activation(root[:], sq[:], ACT.Abs_reciprocal_sqrt, bias=half_c[:])
+            return root
+
+        def hidden(h, qu, root):
+            hid = keep.tile([P, P, PACK], BF16, name="hid" + str(h), align_bytes=64)
+            nc.vector.tensor_tensor(
+                hid[:].rearrange("p (a b) t -> p a t b", b=4),
+                qu[:].rearrange("p t (a b) -> p a t b", b=4),
+                root[:].rearrange("p t (a b) -> p a t b", b=4),
+                ALU.mult,
+            )
+            return quantise("hid" + str(h), hid[:].rearrange("p v t -> p (v t)"), P, 1)
+
+        def scores(h, hid_q):
+            sc = keep.tile([P, Z], F32, name="sc" + str(h))
+            grp = keep.tile([P, Z // 4], F32, name="grp" + str(h))
+            banks = [psum.tile([P, HALF], F32, name="sc_ps", tag="a" + str(2 * h + c)) for c in range(2)]
+            for c in range(2):
+                product(banks[c][:], hid_q, block(0, P), eq, block(c, HALF))
+            for c in range(2):
+                nc.vector.tensor_reduce(
+                    grp[:, block(c, 64)], banks[c][:].rearrange("p (z d) -> p z d", d=4), AX.X, ALU.add
+                )
+                nc.scalar.copy(sc[:, block(1 - c, HALF)], banks[1 - c][:])
+            excl = keep.tile([P, Z], F32, name="excl" + str(h))
+            nc.vector.scalar_tensor_tensor(
+                excl[:].rearrange("p (z d) -> p z d", d=4),
+                grp[:].unsqueeze(2).to_broadcast([P, Z // 4, 4]),
+                -0.2,
+                sc[:].rearrange("p (z d) -> p z d", d=4),
+                ALU.mult,
+                ALU.add,
+            )
+            xm = keep.tile([P, Z], F32, name="xm" + str(h))
+            for c in range(2):
+                cols = block(c, HALF)
+                nc.vector.tensor_tensor(xm[:, cols], excl[:, cols], strict[:, cols], ALU.mult)
+            return sc, xm
+
+        def finish(h, sc, xm, fused):
+            gate = keep.tile([P, Z], F32, name="gate" + str(h))
+            res = keep.tile([P, Z], F32, name="res" + str(h))
+            if not fused:
+                broad = keep.tile([P, Z], F32, name="broad" + str(h))
+                for c in range(2):
+                    nc.scalar.activation(broad[:, block(c, HALF)], sc[:].indirect(brd_t[:, block(c, 16)]), ACT.Copy)
+            for c in range(2):
+                cols = block(c, HALF)
+                nc.scalar.activation(gate[:, cols], xm[:, cols], ACT.Sigmoid)
+            for c in range(2):
+                cols = block(c, HALF)
+                other = sc[:].indirect(brd_t[:, block(c, 16)]) if fused else broad[:, cols]
+                nc.vector.tensor_tensor(res[:, cols], other, gate[:, cols], ALU.mult)
+                nc.sync.dma_start(out[block(h, P), cols], res[:, cols])
+
+        for tt in range(2):
+            magnitude(0, tt)
+            larger(0, tt)
+        for t in range(PACK):
+            fetch_syn(1, t, False)
+        qu0 = weigh(0)
+        eq = (gather("eq", e_tab, adk_t, U32), eq_s)
+        for tt in range(2):
+            magnitude(1, tt)
+            larger(1, tt)
+        root0 = inverse_root(0, qu0)
+        strict = keep.tile([P, Z], F32, name="strict")
+        nc.scalar.activation(strict[:], mth_tab[:].indirect(adk_t[:]), ACT.Copy)
+        hid0 = hidden(0, qu0, root0)
+        qu1 = weigh(1)
+        root1 = inverse_root(1, qu1)
+        sc0, xm0 = scores(0, hid0)
+        hid1 = hidden(1, qu1, root1)
+        sc1, xm1 = scores(1, hid1)
+        finish(0, sc0, xm0, True)
+        finish(1, sc1, xm1, False)

@@ -1,6 +1,7 @@
 from contextlib import ExitStack
 
 import concourse.mybir as mybir
+from concourse.masks import make_identity
 
 F32 = mybir.dt.float32
 BF16 = mybir.dt.bfloat16
@@ -43,18 +44,14 @@ def tile_picked_ysponsq_brd_p_kernel(
             nc.sync.dma_start(t[:].bitcast(I32), src[0].rearrange("p n t -> p (n t)").bitcast(I32))
             return t
 
-        def load_weight(name, src):
-            parts = []
-            rows = src.rearrange("(p j) c -> p j c", j=PACK)
-            for c in range(2):
-                t = keep.tile([P, PACK, H // 2], F32, name=name + str(c))
-                nc.sync.dma_start(t[:], rows[:, :, c * (H // 2) : (c + 1) * (H // 2)])
-                parts.append(t)
-            return parts
+        def load_weight(name, src, c0, c1):
+            t = keep.tile([P, PACK, c1 - c0], F32, name=name)
+            nc.sync.dma_start(t[:], src.rearrange("(p j) c -> p j c", j=PACK)[:, :, c0:c1])
+            return t
 
-        def cast_weight(dealt, part, c, copy):
-            src = part[:].rearrange("p j (m t) -> p m j t", t=PACK)
-            dst = dealt[:, :, c * 64 : (c + 1) * 64, :].rearrange("p t m j -> p m j t")
+        def cast_weight(dealt, m0, raw, copy):
+            src = raw.rearrange("p j (m t) -> p m j t", t=PACK)
+            dst = dealt[:, :, m0 : m0 + src.shape[1], :].rearrange("p t m j -> p m j t")
             copy(dst, src)
 
         def quantise(name, src, width, pieces):
@@ -69,8 +66,8 @@ def tile_picked_ysponsq_brd_p_kernel(
                 )
             return codes, scales
 
-        def gather(name, table, offsets, dtype):
-            t = keep.tile([P, S], dtype, name=name, align_bytes=64)
+        def gather(name, table, offsets, dtype, tag=""):
+            t = keep.tile([P, S], dtype, name=name, tag=tag or name, align_bytes=64)
             nc.vector.tensor_copy(t[:], table[:].indirect(offsets[:]))
             return t
 
@@ -88,102 +85,124 @@ def tile_picked_ysponsq_brd_p_kernel(
         def block(i, n):
             return slice(i * n, (i + 1) * n)
 
-        def load_scales(name, src):
-            t = keep.tile([P, TABLE], U8, name=name)
-            for q in range(4):
-                rows = src[0, block(q, 4), :].bitcast(I32).partition_broadcast(8)
-                nc.sync.dma_start(t[block(q, 32), :].bitcast(I32), rows)
-            return t
-
-        xs_tab = load_scales("xs_tab", x_scales)
+        xs_rows = keep.tile([P, TABLE // 4], I32, name="xs_rows")
+        for q in range(4):
+            nc.sync.dma_start(xs_rows[32 * q : 32 * q + 4, :], x_scales[0, block(q, 4), :].bitcast(I32))
         offs_t = load_list("offs_t", offs)
+        adk_t = load_list("adk_t", adk)
+        mth_row = keep.tile([1, TABLE], F32, name="mth_row")
+        nc.sync.dma_start(mth_row[:], mth[0:1, :])
         x_tab = load_words("x_tab", x_words)
-        w2_raw = load_weight("w2_raw", w2)
-        w1_raw = load_weight("w1_raw", w1)
-        syn_t = load_list("syn_t", syn)
+        w2_a = load_weight("w2_a", w2, 0, 384)
+        w2_z = load_weight("w2_z", w2, 384, 512)
         unit_t = keep.tile([P, PACK], F32, name="unit_t")
         nc.sync.dma_start(unit_t[:], unit.rearrange("(p t) o -> p (t o)", t=PACK))
-        adk_t = load_list("adk_t", adk)
-        es_tab = load_scales("es_tab", e_scales)
-        e_tab = load_words("e_tab", e_words)
-        mth_tab = keep.tile([P, TABLE], F32, name="mth_tab")
-        nc.sync.dma_start(mth_tab[:], mth)
+        syn_t = load_list("syn_t", syn)
         brd_t = load_list("brd_t", brd)
+        w1_raw = load_weight("w1_raw", w1, 0, 512)
+        e_tab = load_words("e_tab", e_words)
 
         half_c = keep.tile([P, 1], F32, name="half_c")
         nc.vector.memset(half_c[:], 0.5)
+        xs_tab = keep.tile([P, TABLE], U8, name="xs_tab")
+        nc.vector.memset(xs_tab[:].bitcast(I32), 0)
+        mth_tab = keep.tile([P, TABLE], F32, name="mth_tab")
+        nc.gpsimd.memset(mth_tab[:], 0.0)
+        es_tab = keep.tile([P, TABLE], U8, name="es_tab")
+        nc.vector.memset(es_tab[:].bitcast(I32), 0)
+        for q in range(4):
+            nc.sync.dma_start(es_tab[32 * q : 32 * q + 4, :].bitcast(I32), e_scales[0, block(q, 4), :].bitcast(I32))
+        ident = keep.tile([P, P], F32, name="ident")
+        make_identity(nc, ident[:])
 
+        warm = keep.tile([P, 1], F32, name="warm")
+        nc.scalar.activation(warm[:], half_c[:], ACT.Abs_reciprocal_sqrt, bias=half_c[:])
+        for q in range(4):
+            nc.vector.tensor_copy(xs_tab[32 * q : 32 * q + 4, :].bitcast(I32), xs_rows[32 * q : 32 * q + 4, :])
+
+        nc.scalar.copy(mth_tab[0:1, :], mth_row[:])
+        strict_row = keep.tile([P, Z], F32, name="strict_row")
+        nc.scalar.activation(strict_row[:], mth_tab[:].indirect(adk_t[:]), ACT.Copy)
         xq_s = gather("xq_s", xs_tab, offs_t, U8)
         xq = (gather("xq", x_tab, offs_t, U32), xq_s)
 
         w2_b = keep.tile([P, PACK, P, PACK], BF16, name="w2_b", align_bytes=64)
-        cast_weight(w2_b, w2_raw[0], 0, nc.scalar.copy)
-        cast_weight(w2_b, w2_raw[1], 1, nc.vector.tensor_copy)
-        w2_q = quantise("w2", w2_b[:].rearrange("p t m j -> p (t m j)"), H, 2)
-
-        yg_ps = [psum.tile([P, S], F32, name="yg_ps", tag="a" + str(t)) for t in range(PACK)]
-        yg_sb = [keep.tile([P, S], F32, name="yg_sb" + str(t)) for t in range(PACK)]
-        gs = [keep.tile([P, PACK, HALF], F32, name="gs" + str(h)) for h in range(2)]
-        for t in range(PACK):
-            product(yg_ps[t][:], w2_q, block(t, P), xq, block(0, S))
-
-        def fetch_syn(h, t, on_vector):
-            window = yg_sb[t][:].indirect(syn_t[:, block(h, 16)])
-            if on_vector:
-                nc.vector.tensor_copy(gs[h][:, t, :], window)
-            else:
-                nc.scalar.activation(gs[h][:, t, :], window, ACT.Copy)
-
-        w1_b = keep.tile([P, PACK, P, PACK], BF16, name="w1_b", align_bytes=64)
-        cast_weight(w1_b, w1_raw[0], 0, nc.vector.tensor_copy)
-        for t in range(PACK):
-            nc.scalar.copy(yg_sb[t][:], yg_ps[t][:])
-        fetch_syn(0, 0, True)
-        cast_weight(w1_b, w1_raw[1], 1, nc.vector.tensor_copy)
+        cast_weight(w2_b, 0, w2_a[:, :, 0:128], nc.scalar.copy)
+        cast_weight(w2_b, 32, w2_a[:, :, 128:384], nc.vector.tensor_copy)
+        cast_weight(w2_b, 96, w2_z[:], nc.vector.tensor_copy)
+        w2_q = quantise("w2", w2_b[:].rearrange("p t m j -> p (t m j)"), H, 4)
 
         u_zero = keep.tile([P, PACK], F32, name="u_zero")
         nc.vector.tensor_scalar(u_zero[:], unit_t[:], 0.0, None, ALU.is_equal)
-        w1_q = quantise("w1", w1_b[:].rearrange("p t m j -> p (t m j)"), H, 2)
         u_safe = keep.tile([P, PACK], F32, name="u_safe")
         nc.vector.tensor_tensor(u_safe[:], u_zero[:], unit_t[:], ALU.add)
-        fetch_syn(0, 1, True)
         u_inv = keep.tile([P, PACK], F32, name="u_inv")
         nc.vector.reciprocal(u_inv[:], u_safe[:])
-        eq_s = gather("eq_s", es_tab, adk_t, U8)
-        fetch_syn(0, 2, False)
-        fetch_syn(0, 3, False)
 
-        best = [keep.tile([P, PACK, HALF], F32, name="best" + str(h)) for h in range(2)]
+        yg_ps = [psum.tile([P, S], F32, name="yg_ps", tag="a" + str(t)) for t in range(PACK)]
+        yg_sb = [keep.tile([P, S], F32, name="yg_sb" + str(t)) for t in range(PACK)]
+        for t in range(PACK):
+            product(yg_ps[t][:], w2_q, block(t, P), xq, block(0, S))
+
+        def fetch_syn(h, tt, on_vector=()):
+            got = keep.tile([P, 2, HALF], F32, name="gs" + str(tt))
+            for i in range(2):
+                window = yg_sb[2 * tt + i][:].indirect(syn_t[:, block(h, 16)])
+                if i in on_vector:
+                    nc.vector.tensor_copy(got[:, i, :], window)
+                else:
+                    nc.scalar.activation(got[:, i, :], window, ACT.Copy)
+            return got
+
+        w1_b = keep.tile([P, PACK, P, PACK], BF16, name="w1_b", align_bytes=64)
+        for t in range(PACK):
+            nc.scalar.copy(yg_sb[t][:], yg_ps[t][:])
+        cast_weight(w1_b, 0, w1_raw[:], nc.vector.tensor_copy)
+
+        w1_q = quantise("w1", w1_b[:].rearrange("p t m j -> p (t m j)"), H, 2)
+
         mag = [keep.tile([P, PACK, HALF], F32, name="mag" + str(h)) for h in range(2)]
         y_ps = [psum.tile([P, 2, HALF], F32, name="y_ps", tag="b" + str(b)) for b in range(4)]
         for h in range(2):
             for t in range(PACK):
                 product(y_ps[2 * h + t // 2][:, t % 2, :], w1_q, block(t, P), xq, block(h, HALF))
 
+        def spread_strictness():
+            turned = psum.tile([P, PACK, P], F32, name="turned", tag="b0")
+            for c in range(PACK):
+                nc.tensor.transpose(turned[:, c, :], strict_row[:, block(c, P)], ident[:])
+            column = keep.tile([P, PACK], F32, name="column")
+            nc.scalar.copy(column[:], turned[:, :, 0])
+            spread = psum.tile([P, Z], F32, name="strict", tag="b1")
+            for c in range(PACK):
+                nc.tensor.transpose(spread[:, block(c, P)], column[:, c : c + 1].to_broadcast([P, P]), ident[:])
+            return spread
+
         def magnitude(h, tt):
             nc.scalar.activation(mag[h][:, block(tt, 2), :], y_ps[2 * h + tt][:], ACT.Abs)
 
-        def larger(h, tt):
-            nc.vector.tensor_tensor(best[h][:, block(tt, 2), :], y_ps[2 * h + tt][:], gs[h][:, block(tt, 2), :], ALU.max)
+        def larger(h, tt, got):
+            best = keep.tile([P, 2, HALF], F32, name="best" + str(2 * h + tt), align_bytes=64)
+            nc.vector.tensor_tensor(best[:], y_ps[2 * h + tt][:], got[:], ALU.max)
+            return best
 
-        def weigh(h):
-            aw = keep.tile([P, PACK, HALF], F32, name="aw" + str(h))
-            qu = keep.tile([P, PACK, P], F32, name="qu" + str(h))
-            for t in range(PACK):
+        aw = [keep.tile([P, PACK, HALF], F32, name="aw" + str(h), align_bytes=64) for h in range(2)]
+        qu = [keep.tile([P, PACK, P], F32, name="qu" + str(h)) for h in range(2)]
+        sq = [keep.tile([P, PACK, P], F32, name="sq" + str(h)) for h in range(2)]
+        root = [keep.tile([P, PACK, P], F32, name="root" + str(h)) for h in range(2)]
+
+        def weigh(h, ts, best):
+            for t in range(ts.start, ts.stop):
                 nc.vector.scalar_tensor_tensor(
-                    aw[:, t, :], best[h][:, t, :], unit_t[:, t : t + 1], mag[h][:, t, :], ALU.mult, ALU.mult
+                    aw[h][:, t, :], best[:, t - ts.start, :], unit_t[:, t : t + 1], mag[h][:, t, :], ALU.mult, ALU.mult
                 )
-            pairs = aw[:].rearrange("p t (v d) -> p t v d", d=2)
-            nc.vector.tensor_tensor(qu[:], pairs[:, :, :, 0], pairs[:, :, :, 1], ALU.add)
-            return qu
+            pairs = aw[h][:, ts, :].rearrange("p t (v d) -> p t v d", d=2)
+            nc.vector.tensor_tensor(qu[h][:, ts, :], pairs[:, :, :, 0], pairs[:, :, :, 1], ALU.add)
 
-        def inverse_root(h, qu):
-            sq = keep.tile([P, PACK, P], F32, name="sq" + str(h))
-            for t in range(PACK):
-                nc.scalar.activation(sq[:, t, :], qu[:, t, :], ACT.Square, scale=u_inv[:, t : t + 1])
-            root = keep.tile([P, PACK, P], F32, name="root" + str(h))
-            nc.scalar.activation(root[:], sq[:], ACT.Abs_reciprocal_sqrt, bias=half_c[:])
-            return root
+        def inverse_root(h, ts):
+            for t in range(ts.start, ts.stop):
+                nc.scalar.activation(sq[h][:, t, :], qu[h][:, t, :], ACT.Square, scale=u_inv[:, t : t + 1])
+            nc.scalar.activation(root[h][:, ts, :], sq[h][:, ts, :], ACT.Abs_reciprocal_sqrt, bias=half_c[:])
 
         def hidden(h, qu, root):
             hid = keep.tile([P, P, PACK], BF16, name="hid" + str(h), align_bytes=64)
@@ -196,65 +215,87 @@ def tile_picked_ysponsq_brd_p_kernel(
             return quantise("hid" + str(h), hid[:].rearrange("p v t -> p (v t)"), P, 1)
 
         def scores(h, hid_q):
-            sc = keep.tile([P, Z], F32, name="sc" + str(h))
-            grp = keep.tile([P, Z // 4], F32, name="grp" + str(h))
             banks = [psum.tile([P, HALF], F32, name="sc_ps", tag="a" + str(2 * h + c)) for c in range(2)]
             for c in range(2):
                 product(banks[c][:], hid_q, block(0, P), eq, block(c, HALF))
+            return banks
+
+        def logits(h, banks):
+            grp = keep.tile([P, Z // 4], F32, name="grp" + str(h))
+            excl = keep.tile([P, Z], F32, name="excl" + str(h))
+            xm = keep.tile([P, Z], F32, name="xm" + str(h))
             for c in range(2):
                 nc.vector.tensor_reduce(
                     grp[:, block(c, 64)], banks[c][:].rearrange("p (z d) -> p z d", d=4), AX.X, ALU.add
                 )
-                nc.scalar.copy(sc[:, block(1 - c, HALF)], banks[1 - c][:])
-            excl = keep.tile([P, Z], F32, name="excl" + str(h))
-            nc.vector.scalar_tensor_tensor(
-                excl[:].rearrange("p (z d) -> p z d", d=4),
-                grp[:].unsqueeze(2).to_broadcast([P, Z // 4, 4]),
-                -0.2,
-                sc[:].rearrange("p (z d) -> p z d", d=4),
-                ALU.mult,
-                ALU.add,
-            )
-            xm = keep.tile([P, Z], F32, name="xm" + str(h))
+            for c in range(2):
+                nc.vector.scalar_tensor_tensor(
+                    excl[:, block(c, HALF)].rearrange("p (z d) -> p z d", d=4),
+                    grp[:, block(c, 64)].unsqueeze(2).to_broadcast([P, 64, 4]),
+                    -0.2,
+                    banks[c][:].rearrange("p (z d) -> p z d", d=4),
+                    ALU.mult,
+                    ALU.add,
+                )
             for c in range(2):
                 cols = block(c, HALF)
                 nc.vector.tensor_tensor(xm[:, cols], excl[:, cols], strict[:, cols], ALU.mult)
-            return sc, xm
+            return xm
 
-        def finish(h, sc, xm, fused):
-            gate = keep.tile([P, Z], F32, name="gate" + str(h))
-            res = keep.tile([P, Z], F32, name="res" + str(h))
-            if not fused:
-                broad = keep.tile([P, Z], F32, name="broad" + str(h))
-                for c in range(2):
-                    nc.scalar.activation(broad[:, block(c, HALF)], sc[:].indirect(brd_t[:, block(c, 16)]), ACT.Copy)
+        def score_rows(h, banks):
+            sc = keep.tile([P, Z], F32, name="sc" + str(h), tag="sq" + str(1 - h))
             for c in range(2):
-                cols = block(c, HALF)
-                nc.scalar.activation(gate[:, cols], xm[:, cols], ACT.Sigmoid)
-            for c in range(2):
-                cols = block(c, HALF)
-                other = sc[:].indirect(brd_t[:, block(c, 16)]) if fused else broad[:, cols]
-                nc.vector.tensor_tensor(res[:, cols], other, gate[:, cols], ALU.mult)
-                nc.sync.dma_start(out[block(h, P), cols], res[:, cols])
+                nc.scalar.copy(sc[:, block(c, HALF)], banks[c][:])
+            return sc
 
+        gate = [keep.tile([P, Z], F32, name="gate" + str(h)) for h in range(2)]
+        res = [keep.tile([P, Z], F32, name="res" + str(h)) for h in range(2)]
+
+        def broader(h, c, sc):
+            broad = keep.tile([P, HALF], F32, name="broad" + str(2 * h + c))
+            nc.scalar.activation(broad[:], sc[:].indirect(brd_t[:, block(c, 16)]), ACT.Copy)
+            return broad[:]
+
+        def squash(h, c, xm):
+            nc.scalar.activation(gate[h][:, block(c, HALF)], xm[:, block(c, HALF)], ACT.Sigmoid)
+
+        def finish(h, c, other):
+            cols = block(c, HALF)
+            nc.vector.tensor_tensor(res[h][:, cols], other, gate[h][:, cols], ALU.mult)
+            nc.sync.dma_start(out[block(h, P), cols], res[h][:, cols])
+
+        eq = (gather("eq", e_tab, adk_t, U32), gather("eq_s", es_tab, adk_t, U8))
+        got = [fetch_syn(0, tt) for tt in range(2)]
         for tt in range(2):
             magnitude(0, tt)
-            larger(0, tt)
-        for t in range(PACK):
-            fetch_syn(1, t, False)
-        qu0 = weigh(0)
-        eq = (gather("eq", e_tab, adk_t, U32), eq_s)
+        best = [larger(0, tt, got[tt]) for tt in range(2)]
+        strict = spread_strictness()
+        got = [fetch_syn(1, tt) for tt in range(2)]
+        for tt in range(2):
+            weigh(0, block(tt, 2), best[tt])
+        best = [larger(1, tt, got[tt]) for tt in range(2)]
+        inverse_root(0, block(0, 4))
         for tt in range(2):
             magnitude(1, tt)
-            larger(1, tt)
-        root0 = inverse_root(0, qu0)
-        strict = keep.tile([P, Z], F32, name="strict")
-        nc.scalar.activation(strict[:], mth_tab[:].indirect(adk_t[:]), ACT.Copy)
-        hid0 = hidden(0, qu0, root0)
-        qu1 = weigh(1)
-        root1 = inverse_root(1, qu1)
-        sc0, xm0 = scores(0, hid0)
-        hid1 = hidden(1, qu1, root1)
-        sc1, xm1 = scores(1, hid1)
-        finish(0, sc0, xm0, True)
-        finish(1, sc1, xm1, False)
+        hid0 = hidden(0, qu[0], root[0])
+        banks0 = scores(0, hid0)
+        for tt in range(2):
+            weigh(1, block(tt, 2), best[tt])
+        for tt in range(2):
+            inverse_root(1, block(tt, 2))
+        sc0 = score_rows(0, banks0)
+        hid1 = hidden(1, qu[1], root[1])
+        banks1 = scores(1, hid1)
+        xm0 = logits(0, banks0)
+        b0 = broader(0, 0, sc0)
+        b1 = broader(0, 1, sc0)
+        squash(0, 0, xm0)
+        squash(0, 1, xm0)
+        xm1 = logits(1, banks1)
+        sc1 = score_rows(1, banks1)
+        finish(0, 0, b0)
+        finish(0, 1, b1)
+        squash(1, 0, xm1)
+        squash(1, 1, xm1)
+        finish(1, 0, sc1[:].indirect(brd_t[:, block(0, 16)]))
+        finish(1, 1, sc1[:].indirect(brd_t[:, block(1, 16)]))

from contextlib import ExitStack

import concourse.mybir as mybir
from concourse.masks import make_identity

F32 = mybir.dt.float32
BF16 = mybir.dt.bfloat16
I32 = mybir.dt.int32
U32 = mybir.dt.uint32
U16 = mybir.dt.uint16
U8 = mybir.dt.uint8
FP8X4 = mybir.dt.float8_e4m3fn_x4
ALU = mybir.AluOpType
ACT = mybir.ActivationFunctionType
AX = mybir.AxisListType

P = 128
PACK = 4
K = 512
TABLE = 2048
S = 512
H = 512
Z = 512
V = 256
HALF = S // 2
FLOPS = 2 * K * H * S * 2 + 2 * H * V * Z


def tile_picked_ysponsq_brd_p_kernel(
    tc, x_words, x_scales, w1, w2, e_words, e_scales, unit, mth, offs, syn, adk, brd, out
):
    nc = tc.nc
    with ExitStack() as ctx:
        keep = ctx.enter_context(tc.tile_pool(name="keep", bufs=1))
        psum = ctx.enter_context(tc.psum_pool(name="psum", bufs=1))

        def load_list(name, src):
            t = keep.tile([P, S // 16], U16, name=name)
            nc.sync.dma_start(t[:], src)
            return t

        def load_words(name, src):
            t = keep.tile([P, TABLE], U32, name=name)
            nc.sync.dma_start(t[:].bitcast(I32), src[0].rearrange("p n t -> p (n t)").bitcast(I32))
            return t

        def load_weight(name, src, c0, c1):
            t = keep.tile([P, PACK, c1 - c0], F32, name=name)
            nc.sync.dma_start(t[:], src.rearrange("(p j) c -> p j c", j=PACK)[:, :, c0:c1])
            return t

        def cast_weight(dealt, m0, raw, copy):
            src = raw.rearrange("p j (m t) -> p m j t", t=PACK)
            dst = dealt[:, :, m0 : m0 + src.shape[1], :].rearrange("p t m j -> p m j t")
            copy(dst, src)

        def quantise(name, src, width, pieces):
            codes = keep.tile([P, width], U32, name=name + "_c", align_bytes=64)
            scales = keep.tile([P, width], U8, name=name + "_s", align_bytes=64)
            n = width // pieces
            for i in range(pieces):
                nc.vector.quantize_mx(
                    out=codes[:, i * n : (i + 1) * n].bitcast(FP8X4),
                    scales=scales[:, i * n : (i + 1) * n],
                    in_=src[:, PACK * i * n : PACK * (i + 1) * n],
                )
            return codes, scales

        def gather(name, table, offsets, dtype, tag=""):
            t = keep.tile([P, S], dtype, name=name, tag=tag or name, align_bytes=64)
            nc.vector.tensor_copy(t[:], table[:].indirect(offsets[:]))
            return t

        def product(dst, lhs, lhs_cols, rhs, rhs_cols):
            nc.tensor.matmul_mx(
                out=dst,
                lhsT=lhs[0][:, lhs_cols].bitcast(FP8X4),
                lhsT_scale=lhs[1][:, lhs_cols],
                rhs=rhs[0][:, rhs_cols].bitcast(FP8X4),
                rhs_scale=rhs[1][:, rhs_cols],
                start=True,
                stop=True,
            )

        def block(i, n):
            return slice(i * n, (i + 1) * n)

        xs_rows = keep.tile([P, TABLE // 4], I32, name="xs_rows")
        for q in range(4):
            nc.sync.dma_start(xs_rows[32 * q : 32 * q + 4, :], x_scales[0, block(q, 4), :].bitcast(I32))
        offs_t = load_list("offs_t", offs)
        adk_t = load_list("adk_t", adk)
        mth_row = keep.tile([1, TABLE], F32, name="mth_row")
        nc.sync.dma_start(mth_row[:], mth[0:1, :])
        x_tab = load_words("x_tab", x_words)
        w2_a = load_weight("w2_a", w2, 0, 384)
        w2_z = load_weight("w2_z", w2, 384, 512)
        unit_t = keep.tile([P, PACK], F32, name="unit_t")
        nc.sync.dma_start(unit_t[:], unit.rearrange("(p t) o -> p (t o)", t=PACK))
        syn_t = load_list("syn_t", syn)
        brd_t = load_list("brd_t", brd)
        w1_raw = load_weight("w1_raw", w1, 0, 512)
        e_tab = load_words("e_tab", e_words)

        half_c = keep.tile([P, 1], F32, name="half_c")
        nc.vector.memset(half_c[:], 0.5)
        xs_tab = keep.tile([P, TABLE], U8, name="xs_tab")
        nc.vector.memset(xs_tab[:].bitcast(I32), 0)
        mth_tab = keep.tile([P, TABLE], F32, name="mth_tab")
        nc.gpsimd.memset(mth_tab[:], 0.0)
        es_tab = keep.tile([P, TABLE], U8, name="es_tab")
        nc.vector.memset(es_tab[:].bitcast(I32), 0)
        for q in range(4):
            nc.sync.dma_start(es_tab[32 * q : 32 * q + 4, :].bitcast(I32), e_scales[0, block(q, 4), :].bitcast(I32))
        ident = keep.tile([P, P], F32, name="ident")
        make_identity(nc, ident[:])

        warm = keep.tile([P, 1], F32, name="warm")
        nc.scalar.activation(warm[:], half_c[:], ACT.Abs_reciprocal_sqrt, bias=half_c[:])
        for q in range(4):
            nc.vector.tensor_copy(xs_tab[32 * q : 32 * q + 4, :].bitcast(I32), xs_rows[32 * q : 32 * q + 4, :])

        nc.scalar.copy(mth_tab[0:1, :], mth_row[:])
        strict_row = keep.tile([P, Z], F32, name="strict_row")
        nc.scalar.activation(strict_row[:], mth_tab[:].indirect(adk_t[:]), ACT.Copy)
        xq_s = gather("xq_s", xs_tab, offs_t, U8)
        xq = (gather("xq", x_tab, offs_t, U32), xq_s)

        w2_b = keep.tile([P, PACK, P, PACK], BF16, name="w2_b", align_bytes=64)
        cast_weight(w2_b, 0, w2_a[:, :, 0:128], nc.scalar.copy)
        cast_weight(w2_b, 32, w2_a[:, :, 128:384], nc.vector.tensor_copy)
        cast_weight(w2_b, 96, w2_z[:], nc.vector.tensor_copy)
        w2_q = quantise("w2", w2_b[:].rearrange("p t m j -> p (t m j)"), H, 4)

        u_zero = keep.tile([P, PACK], F32, name="u_zero")
        nc.vector.tensor_scalar(u_zero[:], unit_t[:], 0.0, None, ALU.is_equal)
        u_safe = keep.tile([P, PACK], F32, name="u_safe")
        nc.vector.tensor_tensor(u_safe[:], u_zero[:], unit_t[:], ALU.add)
        u_inv = keep.tile([P, PACK], F32, name="u_inv")
        nc.vector.reciprocal(u_inv[:], u_safe[:])

        yg_ps = [psum.tile([P, S], F32, name="yg_ps", tag="a" + str(t)) for t in range(PACK)]
        yg_sb = [keep.tile([P, S], F32, name="yg_sb" + str(t)) for t in range(PACK)]
        for t in range(PACK):
            product(yg_ps[t][:], w2_q, block(t, P), xq, block(0, S))

        def fetch_syn(h, tt, on_vector=()):
            got = keep.tile([P, 2, HALF], F32, name="gs" + str(tt))
            for i in range(2):
                window = yg_sb[2 * tt + i][:].indirect(syn_t[:, block(h, 16)])
                if i in on_vector:
                    nc.vector.tensor_copy(got[:, i, :], window)
                else:
                    nc.scalar.activation(got[:, i, :], window, ACT.Copy)
            return got

        w1_b = keep.tile([P, PACK, P, PACK], BF16, name="w1_b", align_bytes=64)
        for t in range(PACK):
            nc.scalar.copy(yg_sb[t][:], yg_ps[t][:])
        cast_weight(w1_b, 0, w1_raw[:], nc.vector.tensor_copy)

        w1_q = quantise("w1", w1_b[:].rearrange("p t m j -> p (t m j)"), H, 2)

        mag = [keep.tile([P, PACK, HALF], F32, name="mag" + str(h)) for h in range(2)]
        y_ps = [psum.tile([P, 2, HALF], F32, name="y_ps", tag="b" + str(b)) for b in range(4)]
        for h in range(2):
            for t in range(PACK):
                product(y_ps[2 * h + t // 2][:, t % 2, :], w1_q, block(t, P), xq, block(h, HALF))

        def spread_strictness():
            turned = psum.tile([P, PACK, P], F32, name="turned", tag="b0")
            for c in range(PACK):
                nc.tensor.transpose(turned[:, c, :], strict_row[:, block(c, P)], ident[:])
            column = keep.tile([P, PACK], F32, name="column")
            nc.scalar.copy(column[:], turned[:, :, 0])
            spread = psum.tile([P, Z], F32, name="strict", tag="b1")
            for c in range(PACK):
                nc.tensor.transpose(spread[:, block(c, P)], column[:, c : c + 1].to_broadcast([P, P]), ident[:])
            return spread

        def magnitude(h, tt):
            nc.scalar.activation(mag[h][:, block(tt, 2), :], y_ps[2 * h + tt][:], ACT.Abs)

        def larger(h, tt, got):
            best = keep.tile([P, 2, HALF], F32, name="best" + str(2 * h + tt), align_bytes=64)
            nc.vector.tensor_tensor(best[:], y_ps[2 * h + tt][:], got[:], ALU.max)
            return best

        aw = [keep.tile([P, PACK, HALF], F32, name="aw" + str(h), align_bytes=64) for h in range(2)]
        qu = [keep.tile([P, PACK, P], F32, name="qu" + str(h)) for h in range(2)]
        sq = [keep.tile([P, PACK, P], F32, name="sq" + str(h)) for h in range(2)]
        root = [keep.tile([P, PACK, P], F32, name="root" + str(h)) for h in range(2)]

        def weigh(h, ts, best):
            for t in range(ts.start, ts.stop):
                nc.vector.scalar_tensor_tensor(
                    aw[h][:, t, :], best[:, t - ts.start, :], unit_t[:, t : t + 1], mag[h][:, t, :], ALU.mult, ALU.mult
                )
            pairs = aw[h][:, ts, :].rearrange("p t (v d) -> p t v d", d=2)
            nc.vector.tensor_tensor(qu[h][:, ts, :], pairs[:, :, :, 0], pairs[:, :, :, 1], ALU.add)

        def inverse_root(h, ts):
            for t in range(ts.start, ts.stop):
                nc.scalar.activation(sq[h][:, t, :], qu[h][:, t, :], ACT.Square, scale=u_inv[:, t : t + 1])
            nc.scalar.activation(root[h][:, ts, :], sq[h][:, ts, :], ACT.Abs_reciprocal_sqrt, bias=half_c[:])

        def hidden(h, qu, root):
            hid = keep.tile([P, P, PACK], BF16, name="hid" + str(h), align_bytes=64)
            nc.vector.tensor_tensor(
                hid[:].rearrange("p (a b) t -> p a t b", b=4),
                qu[:].rearrange("p t (a b) -> p a t b", b=4),
                root[:].rearrange("p t (a b) -> p a t b", b=4),
                ALU.mult,
            )
            return quantise("hid" + str(h), hid[:].rearrange("p v t -> p (v t)"), P, 1)

        def scores(h, hid_q):
            banks = [psum.tile([P, HALF], F32, name="sc_ps", tag="a" + str(2 * h + c)) for c in range(2)]
            for c in range(2):
                product(banks[c][:], hid_q, block(0, P), eq, block(c, HALF))
            return banks

        def logits(h, banks):
            grp = keep.tile([P, Z // 4], F32, name="grp" + str(h))
            excl = keep.tile([P, Z], F32, name="excl" + str(h))
            xm = keep.tile([P, Z], F32, name="xm" + str(h))
            for c in range(2):
                nc.vector.tensor_reduce(
                    grp[:, block(c, 64)], banks[c][:].rearrange("p (z d) -> p z d", d=4), AX.X, ALU.add
                )
            for c in range(2):
                nc.vector.scalar_tensor_tensor(
                    excl[:, block(c, HALF)].rearrange("p (z d) -> p z d", d=4),
                    grp[:, block(c, 64)].unsqueeze(2).to_broadcast([P, 64, 4]),
                    -0.2,
                    banks[c][:].rearrange("p (z d) -> p z d", d=4),
                    ALU.mult,
                    ALU.add,
                )
            for c in range(2):
                cols = block(c, HALF)
                nc.vector.tensor_tensor(xm[:, cols], excl[:, cols], strict[:, cols], ALU.mult)
            return xm

        def score_rows(h, banks):
            sc = keep.tile([P, Z], F32, name="sc" + str(h), tag="sq" + str(1 - h))
            for c in range(2):
                nc.scalar.copy(sc[:, block(c, HALF)], banks[c][:])
            return sc

        gate = [keep.tile([P, Z], F32, name="gate" + str(h)) for h in range(2)]
        res = [keep.tile([P, Z], F32, name="res" + str(h)) for h in range(2)]

        def broader(h, c, sc):
            broad = keep.tile([P, HALF], F32, name="broad" + str(2 * h + c))
            nc.scalar.activation(broad[:], sc[:].indirect(brd_t[:, block(c, 16)]), ACT.Copy)
            return broad[:]

        def squash(h, c, xm):
            nc.scalar.activation(gate[h][:, block(c, HALF)], xm[:, block(c, HALF)], ACT.Sigmoid)

        def finish(h, c, other):
            cols = block(c, HALF)
            nc.vector.tensor_tensor(res[h][:, cols], other, gate[h][:, cols], ALU.mult)
            nc.sync.dma_start(out[block(h, P), cols], res[h][:, cols])

        eq = (gather("eq", e_tab, adk_t, U32), gather("eq_s", es_tab, adk_t, U8))
        got = [fetch_syn(0, tt) for tt in range(2)]
        for tt in range(2):
            magnitude(0, tt)
        best = [larger(0, tt, got[tt]) for tt in range(2)]
        strict = spread_strictness()
        got = [fetch_syn(1, tt) for tt in range(2)]
        for tt in range(2):
            weigh(0, block(tt, 2), best[tt])
        best = [larger(1, tt, got[tt]) for tt in range(2)]
        inverse_root(0, block(0, 4))
        for tt in range(2):
            magnitude(1, tt)
        hid0 = hidden(0, qu[0], root[0])
        banks0 = scores(0, hid0)
        for tt in range(2):
            weigh(1, block(tt, 2), best[tt])
        for tt in range(2):
            inverse_root(1, block(tt, 2))
        sc0 = score_rows(0, banks0)
        hid1 = hidden(1, qu[1], root[1])
        banks1 = scores(1, hid1)
        xm0 = logits(0, banks0)
        b0 = broader(0, 0, sc0)
        b1 = broader(0, 1, sc0)
        squash(0, 0, xm0)
        squash(0, 1, xm0)
        xm1 = logits(1, banks1)
        sc1 = score_rows(1, banks1)
        finish(0, 0, b0)
        finish(0, 1, b1)
        squash(1, 0, xm1)
        squash(1, 1, xm1)
        finish(1, 0, sc1[:].indirect(brd_t[:, block(0, 16)]))
        finish(1, 1, sc1[:].indirect(brd_t[:, block(1, 16)]))
